import numpy as np, ml_dtypes
CORES = [78,86,94,102,110,118]
N = 6
KB, QP = 1, 128
def setup_inputs(rng):
    q = rng.standard_normal((N, 128, QP), dtype=np.float32) / 4; k = rng.standard_normal((N, 128, KB * 128), dtype=np.float32)
    a = 2 * np.pi * rng.random((N, QP)); s = 400 * rng.random((N, QP)) ** 1.5; q[:, 0, :] = s * np.cos(a); q[:, 1, :] = s * np.sin(a); q[:, 2, :] = 150 * rng.standard_normal((N, QP)); k[:, 2, :] = 1 + k[:, 2, :] / 50
    a = (2 * np.pi * rng.random() + np.pi / 2 * (rng.permutation(N).reshape(N, 1, 1) + 0.5) / N - 0.5 + (np.arange(KB).reshape(1, KB, 1) + rng.random((N, KB, 128))) / KB).reshape(N, KB * 128); k[:, 0, :] = np.cos(a); k[:, 1, :] = np.sin(a)
    return {"q": q.astype(ml_dtypes.bfloat16), "k": k.astype(ml_dtypes.bfloat16), "v": rng.standard_normal((N, 128, KB * 128), dtype=np.float32).astype(ml_dtypes.bfloat16)}
def setup_inputs_big(rng):
    d = setup_inputs(rng)
    for k in ("v",): d[k] = (d[k].astype(np.float32) * 1048576.0).astype(d[k].dtype)
    return d
def setup_inputs_small(rng):
    d = setup_inputs(rng)
    for k in ("v",): d[k] = (d[k].astype(np.float32) * (1 / 1048576.0)).astype(d[k].dtype)
    return d
def reference(q, k, v):
    Q, K, V = q.astype(np.float64), k.astype(np.float64), v.astype(np.float64)
    y = np.zeros((N, QP, 128))
    for r in range(N):
        js = list(range(r + 1))
        S = np.concatenate([K[j].T @ Q[r] for j in js], axis=0)
        kp = np.concatenate([j * KB * 128 + np.arange(KB * 128) for j in js]); S = np.where(kp[:, None] <= (r * QP + np.arange(QP))[None, :], S, -np.inf)
        P = np.exp(S - S.max(axis=0)); P = P / P.sum(axis=0)
        y[r] = P.T @ np.concatenate([V[j][:, 128 * b:128 * b + 128] for j in js for b in range(KB)], axis=0)
    return {"y": y.astype(ml_dtypes.bfloat16)}

@@ -1,0 +1,173 @@
+from concourse.bass import DstId, RemoteDMATransfer
+from concourse.mybir import AluOpType, AxisListType, ActivationFunctionType
+
+NR = 6
+SLOT = 256
+
+SCRATCH = {
+    "kv": ("sbuf", [128, NR * SLOT], "bfloat16"),
+    "qs": ("sbuf", [128, 128], "bfloat16"),
+    "dm": ("sbuf", [128, 128], "bfloat16"),
+    "ident": ("sbuf", [128, 128], "bfloat16"),
+    "maskT": ("sbuf", [128, 128], "bfloat16"),
+    "pt": ("sbuf", [128, NR * 128], "bfloat16"),
+    "pp": ("sbuf", [128, NR * 128], "bfloat16"),
+    "da": ("sbuf", [128, NR * 128], "bfloat16"),
+    "osb": ("sbuf", [128, NR * 128], "bfloat16"),
+    "ysb": ("sbuf", [128, 128], "bfloat16"),
+    "nbm": ("sbuf", [128, 8], "float32"),
+    "nM": ("sbuf", [128, 8], "float32"),
+    "av": ("sbuf", [128, 8], "float32"),
+    "lv": ("sbuf", [128, 8], "float32"),
+    "Lv": ("sbuf", [128, 8], "float32"),
+    "rl": ("sbuf", [128, 4], "float32"),
+    "st0": ("psum", [128, 512], "float32"),
+    "st1": ("psum", [128, 512], "float32"),
+    "tr0": ("psum", [128, 1024], "bfloat16"),
+    "tr1": ("psum", [128, 1024], "bfloat16"),
+    "o0": ("psum", [128, 512], "float32"),
+    "o1": ("psum", [128, 512], "float32"),
+}
+STAGES = ["st", "bm", "m", "p", "a", "da", "tr", "c", "o", "os", "L"]
+SEMAPHORES = (["iot", "idn", "msk", "kvl", "ql", "sent", "rc", "yy", "sto"]
+              + ["arr%d" % j for j in range(NR)]
+              + [s + str(t) for s in STAGES for t in range(NR)])
+
+
+def rank_program(g, core, T, topo):
+    r = T.rank_of(core)
+    if r is None:
+        return
+    pe, dve, act, sp = g.tensor, g.vector, g.scalar, g.sync
+    S = T.sem
+    EXP, COPY = ActivationFunctionType.Exp, ActivationFunctionType.Copy
+    cores = list(T.cores)
+
+    def send_mask(j):
+        m = None
+        for d in cores[j + 1:]:
+            if not topo.may_write(cores[j], d):
+                raise ValueError("rank %d may not write to core %d" % (j, d))
+            m = topo.mask(cores[j], d) if m is None else (m & topo.mask(cores[j], d))
+        return m
+
+    def engines(m):
+        return bin(m).count("1")
+
+    def slot(j):
+        return T.kv[:, j * SLOT:(j + 1) * SLOT]
+
+    def kcol(j):
+        return T.kv[:, j * SLOT:j * SLOT + 128]
+
+    def vcol(j):
+        return T.kv[:, j * SLOT + 128:j * SLOT + 256]
+
+    def blk(buf, t):
+        return buf[:, t * 128:(t + 1) * 128]
+
+    def col(buf, t):
+        return buf[:, t:t + 1]
+
+    def ev(stage, t):
+        return S[stage + str(t)]
+
+    sp.dma_start(kcol(r), T.k[:]).then_inc(S.kvl, 16)
+    act.dma_start(vcol(r), T.v[:]).then_inc(S.kvl, 16)
+    sp.dma_start(T.qs[:], T.q[:]).then_inc(S.ql, 16)
+
+    g.iota(T.dm[:], [[1, 128]], 0, -1, allow_small_or_imprecise_dtypes=True).then_inc(S.iot, 1)
+    later = cores[r + 1:]
+    if later:
+        m = send_mask(r)
+        ids = []
+        for d in later:
+            rid, pid, _se = topo.addr(d)
+            ids.append(DstId(rid=rid, pnc=pid))
+        g.wait_ge(S.kvl, 32)
+        g.remote_dma_fused(
+            [RemoteDMATransfer(dst_ids=ids, dma_engine_mask=m, remote_sem=S["arr%d" % r],
+                               srcs=[slot(r)], dsts=[slot(r) for _d in later])],
+            local_sem=S.sent)
+
+    order = [r - t for t in range(r + 1)]
+    last = r
+    ST = [T.st0, T.st1]
+    TR = [T.tr0, T.tr1]
+    OO = [T.o0, T.o1]
+
+    dve.wait_ge(S.iot, 1)
+    dve.tensor_scalar(T.ident[:], T.dm[:], 0.0, None, AluOpType.is_equal).then_inc(S.idn, 1)
+    dve.tensor_scalar(T.maskT[:], T.dm[:], 0.0, -30000.0, AluOpType.is_gt, AluOpType.mult).then_inc(S.msk, 1)
+
+    def pe_scores(t):
+        j = order[t]
+        out = ST[t % 2][:, 0:128]
+        if t == 0:
+            pe.wait_ge(S.kvl, 32)
+            pe.wait_ge(S.ql, 16)
+            pe.matmul(out, T.qs[:], kcol(j), True, False)
+            pe.wait_ge(S.idn, 1)
+            pe.wait_ge(S.msk, 1)
+            pe.matmul(out, T.ident[:], T.maskT[:], False, True).then_inc(ev("st", t), 1)
+        else:
+            pe.wait_ge(S["arr%d" % j], engines(send_mask(j)))
+            if t >= 2:
+                pe.wait_ge(ev("m", 0) if t == 2 else ev("bm", t - 2), 1)
+            pe.matmul(out, T.qs[:], kcol(j), True, True).then_inc(ev("st", t), 1)
+
+    pe_scores(0)
+    for t in range(last + 1):
+        j = order[t]
+        st = ST[t % 2][:, 0:128]
+        tr = TR[t % 2][:, 0:128]
+        oo = OO[t % 2][:, 0:128]
+        dve.wait_ge(ev("st", t), 1)
+        if t == 0:
+            dve.tensor_reduce(col(T.nM, 0), st, AxisListType.X, AluOpType.max, negate=True).then_inc(ev("m", 0), 1)
+        else:
+            dve.tensor_reduce(col(T.nbm, t), st, AxisListType.X, AluOpType.max, negate=True).then_inc(ev("bm", t), 1)
+            dve.wait_ge(ev("bm", t), 1)
+            dve.tensor_tensor(col(T.nM, t), col(T.nM, t - 1), col(T.nbm, t), AluOpType.min).then_inc(ev("m", t), 1)
+        act.wait_ge(ev("m", t), 1)
+        act.activation(blk(T.pt, t), st, EXP, bias=col(T.nM, t), scale=1.0,
+                       accum_out=col(T.Lv, 0) if t == 0 else col(T.lv, t)).then_inc(ev("p", t), 1)
+        if t > 0:
+            act.activation(col(T.av, t), col(T.nM, t - 1), EXP, bias=col(T.nM, t), scale=-1.0).then_inc(ev("a", t), 1)
+        pe.wait_ge(ev("p", t), 1)
+        pe.transpose(tr, blk(T.pt, t), T.ident[:]).then_inc(ev("tr", t), 1)
+        if t < last:
+            pe_scores(t + 1)
+        act.wait_ge(ev("tr", t), 1)
+        act.activation(blk(T.pp, t), tr, COPY).then_inc(ev("c", t), 1)
+        if t > 0:
+            dve.wait_ge(ev("o", t - 1), 1)
+            dve.tensor_copy(blk(T.osb, t - 1), OO[(t - 1) % 2][:, 0:128]).then_inc(ev("os", t - 1), 1)
+            dve.wait_ge(ev("a", t), 1)
+            if t == 1:
+                dve.wait_ge(S.idn, 1)
+            dve.tensor_scalar(blk(T.da, t), T.ident[:], col(T.av, t), None, AluOpType.mult).then_inc(ev("da", t), 1)
+            dve.wait_ge(ev("p", t), 1)
+            if t == 1:
+                dve.wait_ge(ev("p", 0), 1)
+            else:
+                dve.wait_ge(ev("L", t - 1), 1)
+            dve.tensor_scalar(col(T.Lv, t), col(T.Lv, t - 1), col(T.av, t), col(T.lv, t),
+                              AluOpType.mult, AluOpType.add).then_inc(ev("L", t), 1)
+        if t > 0:
+            pe.wait_ge(ev("da", t), 1)
+            pe.wait_ge(ev("os", t - 1), 1)
+            pe.matmul(oo, blk(T.da, t), blk(T.osb, t - 1), True, False)
+        pe.wait_ge(ev("c", t), 1)
+        pe.matmul(oo, blk(T.pp, t), vcol(j), t == 0, True).then_inc(ev("o", t), 1)
+
+    dve.wait_ge(ev("p", 0) if last == 0 else ev("L", last), 1)
+    dve.reciprocal(col(T.rl, 0), col(T.Lv, last)).then_inc(S.rc, 1)
+    dve.wait_ge(S.rc, 1)
+    dve.wait_ge(ev("o", last), 1)
+    dve.tensor_scalar(T.ysb[:], OO[last % 2][:, 0:128], col(T.rl, 0), None, AluOpType.mult).then_inc(S.yy, 1)
+    sp.wait_ge(S.yy, 1)
+    sp.dma_start(T.y[:], T.ysb[:]).then_inc(S.sto, 16)
+    sp.wait_ge(S.sto, 16)
+    if later:
+        g.wait_ge(S.sent, engines(send_mask(r)))

@@ -12,26 +12,29 @@ SCRATCH = {
     "maskT": ("sbuf", [128, 128], "bfloat16"),
     "pt": ("sbuf", [128, NR * 128], "bfloat16"),
     "pp": ("sbuf", [128, NR * 128], "bfloat16"),
-    "da": ("sbuf", [128, NR * 128], "bfloat16"),
-    "osb": ("sbuf", [128, NR * 128], "bfloat16"),
+    "da": ("sbuf", [128, 128], "bfloat16"),
+    "osb": ("sbuf", [128, 128], "bfloat16"),
     "ysb": ("sbuf", [128, 128], "bfloat16"),
-    "nbm": ("sbuf", [128, 8], "float32"),
-    "nM": ("sbuf", [128, 8], "float32"),
-    "av": ("sbuf", [128, 8], "float32"),
+    "nb": ("sbuf", [128, 8], "float32"),
+    "nM": ("sbuf", [128, 4], "float32"),
+    "av": ("sbuf", [128, 4], "float32"),
     "lv": ("sbuf", [128, 8], "float32"),
-    "Lv": ("sbuf", [128, 8], "float32"),
+    "L0": ("sbuf", [128, 4], "float32"),
+    "Lf": ("sbuf", [128, 4], "float32"),
     "rl": ("sbuf", [128, 4], "float32"),
     "st0": ("psum", [128, 512], "float32"),
     "st1": ("psum", [128, 512], "float32"),
+    "st2": ("psum", [128, 512], "float32"),
     "tr0": ("psum", [128, 1024], "bfloat16"),
     "tr1": ("psum", [128, 1024], "bfloat16"),
+    "tr2": ("psum", [128, 1024], "bfloat16"),
     "o0": ("psum", [128, 512], "float32"),
     "o1": ("psum", [128, 512], "float32"),
 }
-STAGES = ["st", "bm", "m", "p", "a", "da", "tr", "c", "o", "os", "L"]
-SEMAPHORES = (["iot", "idn", "msk", "kvl", "ql", "sent", "rc", "yy", "sto"]
+SEMAPHORES = (["iot", "idn", "msk", "kvl", "ql", "sent", "rcp", "yy", "sto",
+               "s0", "m0", "p0", "t0", "c0", "og0", "os0", "mm", "aa", "al", "dd", "og1", "ls"]
               + ["arr%d" % j for j in range(NR)]
-              + [s + str(t) for s in STAGES for t in range(NR)])
+              + [s + str(c) for s in ["sc", "rc", "pc", "tc", "cc"] for c in range(3)])
 
 
 def rank_program(g, core, T, topo):
@@ -40,7 +43,8 @@ def rank_program(g, core, T, topo):
         return
     pe, dve, act, sp = g.tensor, g.vector, g.scalar, g.sync
     S = T.sem
-    EXP, COPY = ActivationFunctionType.Exp, ActivationFunctionType.Copy
+    EXP, COPY, IDENT = ActivationFunctionType.Exp, ActivationFunctionType.Copy, ActivationFunctionType.Identity
+    X = AxisListType.X
     cores = list(T.cores)
 
     def send_mask(j):
@@ -63,14 +67,11 @@ def rank_program(g, core, T, topo):
     def vcol(j):
         return T.kv[:, j * SLOT + 128:j * SLOT + 256]
 
-    def blk(buf, t):
-        return buf[:, t * 128:(t + 1) * 128]
+    def cols(buf, a, n):
+        return buf[:, a * 128:(a + n) * 128]
 
     def col(buf, t):
         return buf[:, t:t + 1]
-
-    def ev(stage, t):
-        return S[stage + str(t)]
 
     sp.dma_start(kcol(r), T.k[:]).then_inc(S.kvl, 16)
     act.dma_start(vcol(r), T.v[:]).then_inc(S.kvl, 16)
@@ -79,93 +80,111 @@ def rank_program(g, core, T, topo):
     g.iota(T.dm[:], [[1, 128]], 0, -1, allow_small_or_imprecise_dtypes=True).then_inc(S.iot, 1)
     later = cores[r + 1:]
     if later:
-        m = send_mask(r)
         ids = []
         for d in later:
             rid, pid, _se = topo.addr(d)
             ids.append(DstId(rid=rid, pnc=pid))
         g.wait_ge(S.kvl, 32)
         g.remote_dma_fused(
-            [RemoteDMATransfer(dst_ids=ids, dma_engine_mask=m, remote_sem=S["arr%d" % r],
+            [RemoteDMATransfer(dst_ids=ids, dma_engine_mask=send_mask(r), remote_sem=S["arr%d" % r],
                                srcs=[slot(r)], dsts=[slot(r) for _d in later])],
             local_sem=S.sent)
-
-    order = [r - t for t in range(r + 1)]
-    last = r
-    ST = [T.st0, T.st1]
-    TR = [T.tr0, T.tr1]
-    OO = [T.o0, T.o1]
 
     dve.wait_ge(S.iot, 1)
     dve.tensor_scalar(T.ident[:], T.dm[:], 0.0, None, AluOpType.is_equal).then_inc(S.idn, 1)
     dve.tensor_scalar(T.maskT[:], T.dm[:], 0.0, -30000.0, AluOpType.is_gt, AluOpType.mult).then_inc(S.msk, 1)
 
-    def pe_scores(t):
-        j = order[t]
-        out = ST[t % 2][:, 0:128]
-        if t == 0:
-            pe.wait_ge(S.kvl, 32)
-            pe.wait_ge(S.ql, 16)
-            pe.matmul(out, T.qs[:], kcol(j), True, False)
-            pe.wait_ge(S.idn, 1)
-            pe.wait_ge(S.msk, 1)
-            pe.matmul(out, T.ident[:], T.maskT[:], False, True).then_inc(ev("st", t), 1)
-        else:
-            pe.wait_ge(S["arr%d" % j], engines(send_mask(j)))
-            if t >= 2:
-                pe.wait_ge(ev("m", 0) if t == 2 else ev("bm", t - 2), 1)
-            pe.matmul(out, T.qs[:], kcol(j), True, True).then_inc(ev("st", t), 1)
+    st = T.st0[:, 0:128]
+    pe.wait_ge(S.kvl, 32)
+    pe.wait_ge(S.ql, 16)
+    pe.matmul(st, T.qs[:], kcol(r), True, False)
+    pe.wait_ge(S.idn, 1)
+    pe.wait_ge(S.msk, 1)
+    pe.matmul(st, T.ident[:], T.maskT[:], False, True).then_inc(S.s0, 1)
+    dve.wait_ge(S.s0, 1)
+    dve.tensor_reduce(col(T.nb, 0), st, X, AluOpType.max, negate=True).then_inc(S.m0, 1)
+    act.wait_ge(S.m0, 1)
+    act.activation(cols(T.pt, 0, 1), st, EXP, bias=col(T.nb, 0), scale=1.0, accum_out=col(T.L0, 0)).then_inc(S.p0, 1)
+    pe.wait_ge(S.p0, 1)
+    pe.transpose(T.tr0[:, 0:128], cols(T.pt, 0, 1), T.ident[:]).then_inc(S.t0, 1)
+    act.wait_ge(S.t0, 1)
+    act.activation(cols(T.pp, 0, 1), T.tr0[:, 0:128], COPY).then_inc(S.c0, 1)
+    pe.wait_ge(S.c0, 1)
+    pe.matmul(T.o0[:, 0:128], cols(T.pp, 0, 1), vcol(r), True, True).then_inc(S.og0, 1)
 
-    pe_scores(0)
-    for t in range(last + 1):
-        j = order[t]
-        st = ST[t % 2][:, 0:128]
-        tr = TR[t % 2][:, 0:128]
-        oo = OO[t % 2][:, 0:128]
-        dve.wait_ge(ev("st", t), 1)
-        if t == 0:
-            dve.tensor_reduce(col(T.nM, 0), st, AxisListType.X, AluOpType.max, negate=True).then_inc(ev("m", 0), 1)
-        else:
-            dve.tensor_reduce(col(T.nbm, t), st, AxisListType.X, AluOpType.max, negate=True).then_inc(ev("bm", t), 1)
-            dve.wait_ge(ev("bm", t), 1)
-            dve.tensor_tensor(col(T.nM, t), col(T.nM, t - 1), col(T.nbm, t), AluOpType.min).then_inc(ev("m", t), 1)
-        act.wait_ge(ev("m", t), 1)
-        act.activation(blk(T.pt, t), st, EXP, bias=col(T.nM, t), scale=1.0,
-                       accum_out=col(T.Lv, 0) if t == 0 else col(T.lv, t)).then_inc(ev("p", t), 1)
-        if t > 0:
-            act.activation(col(T.av, t), col(T.nM, t - 1), EXP, bias=col(T.nM, t), scale=-1.0).then_inc(ev("a", t), 1)
-        pe.wait_ge(ev("p", t), 1)
-        pe.transpose(tr, blk(T.pt, t), T.ident[:]).then_inc(ev("tr", t), 1)
-        if t < last:
-            pe_scores(t + 1)
-        act.wait_ge(ev("tr", t), 1)
-        act.activation(blk(T.pp, t), tr, COPY).then_inc(ev("c", t), 1)
-        if t > 0:
-            dve.wait_ge(ev("o", t - 1), 1)
-            dve.tensor_copy(blk(T.osb, t - 1), OO[(t - 1) % 2][:, 0:128]).then_inc(ev("os", t - 1), 1)
-            dve.wait_ge(ev("a", t), 1)
-            if t == 1:
-                dve.wait_ge(S.idn, 1)
-            dve.tensor_scalar(blk(T.da, t), T.ident[:], col(T.av, t), None, AluOpType.mult).then_inc(ev("da", t), 1)
-            dve.wait_ge(ev("p", t), 1)
-            if t == 1:
-                dve.wait_ge(ev("p", 0), 1)
+    if r == 0:
+        dve.wait_ge(S.p0, 1)
+        dve.reciprocal(col(T.rl, 0), col(T.L0, 0)).then_inc(S.rcp, 1)
+        dve.wait_ge(S.rcp, 1)
+        dve.wait_ge(S.og0, 1)
+        dve.tensor_scalar(T.ysb[:], T.o0[:, 0:128], col(T.rl, 0), None, AluOpType.mult).then_inc(S.yy, 1)
+    else:
+        dve.wait_ge(S.og0, 1)
+        dve.tensor_copy(T.osb[:], T.o0[:, 0:128]).then_inc(S.os0, 1)
+
+        steps = list(range(1, r + 1))
+        head = steps[:-1]
+        chunks = [head[i:i + 2] for i in range(0, len(head), 2)] + [steps[-1:]]
+        nc = len(chunks)
+        STB = [T.st1, T.st2, T.st0]
+        TRB = [T.tr1, T.tr2, T.tr0]
+
+        for c, ch in enumerate(chunks):
+            if STB[c] is T.st0:
+                pe.wait_ge(S.m0, 1)
+            for i, t in enumerate(ch):
+                j = r - t
+                pe.wait_ge(S["arr%d" % j], engines(send_mask(j)))
+                pe.matmul(cols(STB[c], i, 1), T.qs[:], kcol(j), True, True).then_inc(S["sc%d" % c], 1)
+            dve.wait_ge(S["sc%d" % c], len(ch))
+            dve.tensor_reduce(col(T.nb, 1 + c), cols(STB[c], 0, len(ch)), X, AluOpType.max,
+                              negate=True).then_inc(S["rc%d" % c], 1)
+        for c in range(nc):
+            dve.wait_ge(S["rc%d" % c], 1)
+        dve.wait_ge(S.m0, 1)
+        dve.tensor_reduce(col(T.nM, 0), T.nb[:, 0:nc + 1], X, AluOpType.min).then_inc(S.mm, 1)
+        act.wait_ge(S.mm, 1)
+        for c, ch in enumerate(chunks):
+            act.activation(cols(T.pt, ch[0], len(ch)), cols(STB[c], 0, len(ch)), EXP, bias=col(T.nM, 0), scale=1.0,
+                           accum_out=col(T.lv, c)).then_inc(S["pc%d" % c], 1)
+            if c == 0:
+                act.activation(col(T.av, 0), col(T.nb, 0), EXP, bias=col(T.nM, 0), scale=-1.0).then_inc(S.aa, 1)
+            if c == min(1, nc - 1):
+                act.wait_ge(S.aa, 1)
+                act.activation(col(T.lv, nc), col(T.L0, 0), IDENT, scale=col(T.av, 0)).then_inc(S.al, 1)
+        for c, ch in enumerate(chunks):
+            pe.wait_ge(S["pc%d" % c], 1)
+            for i, t in enumerate(ch):
+                pe.transpose(cols(TRB[c], i, 1), cols(T.pt, t, 1), T.ident[:]).then_inc(S["tc%d" % c], 1)
+        dve.wait_ge(S.aa, 1)
+        dve.wait_ge(S.idn, 1)
+        dve.tensor_scalar(T.da[:], T.ident[:], col(T.av, 0), None, AluOpType.mult).then_inc(S.dd, 1)
+        for c, ch in enumerate(chunks):
+            q = act if c == nc - 1 else dve
+            q.wait_ge(S["tc%d" % c], len(ch))
+            if c == nc - 1:
+                act.activation(cols(T.pp, ch[0], len(ch)), cols(TRB[c], 0, len(ch)), COPY).then_inc(S["cc%d" % c], 1)
             else:
-                dve.wait_ge(ev("L", t - 1), 1)
-            dve.tensor_scalar(col(T.Lv, t), col(T.Lv, t - 1), col(T.av, t), col(T.lv, t),
-                              AluOpType.mult, AluOpType.add).then_inc(ev("L", t), 1)
-        if t > 0:
-            pe.wait_ge(ev("da", t), 1)
-            pe.wait_ge(ev("os", t - 1), 1)
-            pe.matmul(oo, blk(T.da, t), blk(T.osb, t - 1), True, False)
-        pe.wait_ge(ev("c", t), 1)
-        pe.matmul(oo, blk(T.pp, t), vcol(j), t == 0, True).then_inc(ev("o", t), 1)
+                dve.tensor_copy(cols(T.pp, ch[0], len(ch)), cols(TRB[c], 0, len(ch))).then_inc(S["cc%d" % c], 1)
+        pe.wait_ge(S.dd, 1)
+        pe.wait_ge(S.os0, 1)
+        pe.matmul(T.o1[:, 0:128], T.da[:], T.osb[:], True, False)
+        for c, ch in enumerate(chunks):
+            pe.wait_ge(S["cc%d" % c], 1)
+            for t in ch:
+                mmi = pe.matmul(T.o1[:, 0:128], cols(T.pp, t, 1), vcol(r - t), False, t == r)
+                if t == r:
+                    mmi.then_inc(S.og1, 1)
+        for c in range(nc):
+            dve.wait_ge(S["pc%d" % c], 1)
+        dve.wait_ge(S.al, 1)
+        dve.tensor_reduce(col(T.Lf, 0), T.lv[:, 0:nc + 1], X, AluOpType.add).then_inc(S.ls, 1)
+        dve.wait_ge(S.ls, 1)
+        dve.reciprocal(col(T.rl, 0), col(T.Lf, 0)).then_inc(S.rcp, 1)
+        dve.wait_ge(S.rcp, 1)
+        dve.wait_ge(S.og1, 1)
+        dve.tensor_scalar(T.ysb[:], T.o1[:, 0:128], col(T.rl, 0), None, AluOpType.mult).then_inc(S.yy, 1)
 
-    dve.wait_ge(ev("p", 0) if last == 0 else ev("L", last), 1)
-    dve.reciprocal(col(T.rl, 0), col(T.Lv, last)).then_inc(S.rc, 1)
-    dve.wait_ge(S.rc, 1)
-    dve.wait_ge(ev("o", last), 1)
-    dve.tensor_scalar(T.ysb[:], OO[last % 2][:, 0:128], col(T.rl, 0), None, AluOpType.mult).then_inc(S.yy, 1)
     sp.wait_ge(S.yy, 1)
     sp.dma_start(T.y[:], T.ysb[:]).then_inc(S.sto, 16)
     sp.wait_ge(S.sto, 16)

@@ -7,20 +7,21 @@ SLOT = 256
 SCRATCH = {
     "kv": ("sbuf", [128, NR * SLOT], "bfloat16"),
     "qs": ("sbuf", [128, 128], "bfloat16"),
+    "qn": ("sbuf", [128, 128], "bfloat16"),
     "dm": ("sbuf", [128, 128], "bfloat16"),
     "ident": ("sbuf", [128, 128], "bfloat16"),
     "maskT": ("sbuf", [128, 128], "bfloat16"),
+    "zz": ("sbuf", [128, 256], "float32"),
+    "scn": ("sbuf", [128, 3 * 256], "float32"),
     "pt": ("sbuf", [128, NR * 128], "bfloat16"),
     "pp": ("sbuf", [128, NR * 128], "bfloat16"),
-    "da": ("sbuf", [128, 128], "bfloat16"),
-    "osb": ("sbuf", [128, 128], "bfloat16"),
+    "da": ("sbuf", [128, 3 * 128], "bfloat16"),
+    "osb": ("sbuf", [128, 3 * 128], "bfloat16"),
     "ysb": ("sbuf", [128, 128], "bfloat16"),
-    "nb": ("sbuf", [128, 8], "float32"),
-    "nM": ("sbuf", [128, 4], "float32"),
+    "nb": ("sbuf", [128, 4], "float32"),
     "av": ("sbuf", [128, 4], "float32"),
-    "lv": ("sbuf", [128, 8], "float32"),
-    "L0": ("sbuf", [128, 4], "float32"),
-    "Lf": ("sbuf", [128, 4], "float32"),
+    "lv": ("sbuf", [128, 24], "float32"),
+    "Lg": ("sbuf", [128, 4], "float32"),
     "rl": ("sbuf", [128, 4], "float32"),
     "st0": ("psum", [128, 512], "float32"),
     "st1": ("psum", [128, 512], "float32"),
@@ -31,10 +32,10 @@ SCRATCH = {
     "o0": ("psum", [128, 512], "float32"),
     "o1": ("psum", [128, 512], "float32"),
 }
-SEMAPHORES = (["iot", "idn", "msk", "kvl", "ql", "sent", "rcp", "yy", "sto",
-               "s0", "m0", "p0", "t0", "c0", "og0", "os0", "mm", "aa", "al", "dd", "og1", "ls"]
+SEMAPHORES = (["iot", "idn", "msk", "zer", "qng", "kvl", "ql", "sent", "rcp", "yy", "sto", "s0", "m0"]
               + ["arr%d" % j for j in range(NR)]
-              + [s + str(c) for s in ["sc", "rc", "pc", "tc", "cc"] for c in range(3)])
+              + [s + str(t) for s in ["ex", "tt", "cp"] for t in range(NR)]
+              + [s + str(c) for s in ["sc", "rc", "ga", "gl", "gd", "go", "gs", "gL"] for c in range(3)])
 
 
 def rank_program(g, core, T, topo):
@@ -45,6 +46,7 @@ def rank_program(g, core, T, topo):
     S = T.sem
     EXP, COPY, IDENT = ActivationFunctionType.Exp, ActivationFunctionType.Copy, ActivationFunctionType.Identity
     X = AxisListType.X
+    MIN, ADD = AluOpType.min, AluOpType.add
     cores = list(T.cores)
 
     def send_mask(j):
@@ -73,6 +75,9 @@ def rank_program(g, core, T, topo):
     def col(buf, t):
         return buf[:, t:t + 1]
 
+    def ev(name, i):
+        return S[name + str(i)]
+
     sp.dma_start(kcol(r), T.k[:]).then_inc(S.kvl, 16)
     act.dma_start(vcol(r), T.v[:]).then_inc(S.kvl, 16)
     sp.dma_start(T.qs[:], T.q[:]).then_inc(S.ql, 16)
@@ -90,9 +95,12 @@ def rank_program(g, core, T, topo):
                                srcs=[slot(r)], dsts=[slot(r) for _d in later])],
             local_sem=S.sent)
 
+    dve.memset(T.zz[:], 0.0).then_inc(S.zer, 1)
     dve.wait_ge(S.iot, 1)
     dve.tensor_scalar(T.ident[:], T.dm[:], 0.0, None, AluOpType.is_equal).then_inc(S.idn, 1)
     dve.tensor_scalar(T.maskT[:], T.dm[:], 0.0, -30000.0, AluOpType.is_gt, AluOpType.mult).then_inc(S.msk, 1)
+    dve.wait_ge(S.ql, 16)
+    dve.tensor_scalar(T.qn[:], T.qs[:], -1.0, None, AluOpType.mult).then_inc(S.qng, 1)
 
     st = T.st0[:, 0:128]
     pe.wait_ge(S.kvl, 32)
@@ -104,87 +112,155 @@ def rank_program(g, core, T, topo):
     dve.wait_ge(S.s0, 1)
     dve.tensor_reduce(col(T.nb, 0), st, X, AluOpType.max, negate=True).then_inc(S.m0, 1)
     act.wait_ge(S.m0, 1)
-    act.activation(cols(T.pt, 0, 1), st, EXP, bias=col(T.nb, 0), scale=1.0, accum_out=col(T.L0, 0)).then_inc(S.p0, 1)
-    pe.wait_ge(S.p0, 1)
-    pe.transpose(T.tr0[:, 0:128], cols(T.pt, 0, 1), T.ident[:]).then_inc(S.t0, 1)
-    act.wait_ge(S.t0, 1)
-    act.activation(cols(T.pp, 0, 1), T.tr0[:, 0:128], COPY).then_inc(S.c0, 1)
-    pe.wait_ge(S.c0, 1)
-    pe.matmul(T.o0[:, 0:128], cols(T.pp, 0, 1), vcol(r), True, True).then_inc(S.og0, 1)
+    act.activation(cols(T.pt, 0, 1), st, EXP, bias=col(T.nb, 0), scale=1.0,
+                   accum_out=col(T.Lg, 0)).then_inc(S.ex0, 1)
+    pe.wait_ge(S.ex0, 1)
+    pe.transpose(T.tr0[:, 0:128], cols(T.pt, 0, 1), T.ident[:]).then_inc(S.tt0, 1)
+    act.wait_ge(S.tt0, 1)
+    act.activation(cols(T.pp, 0, 1), T.tr0[:, 0:128], COPY).then_inc(S.cp0, 1)
+    pe.wait_ge(S.cp0, 1)
+    pe.matmul(T.o0[:, 0:128], cols(T.pp, 0, 1), vcol(r), True, True).then_inc(S.go0, 1)
+    pe.wait_ge(S.qng, 1)
 
-    if r == 0:
-        dve.wait_ge(S.p0, 1)
-        dve.reciprocal(col(T.rl, 0), col(T.L0, 0)).then_inc(S.rcp, 1)
-        dve.wait_ge(S.rcp, 1)
-        dve.wait_ge(S.og0, 1)
-        dve.tensor_scalar(T.ysb[:], T.o0[:, 0:128], col(T.rl, 0), None, AluOpType.mult).then_inc(S.yy, 1)
-    else:
-        dve.wait_ge(S.og0, 1)
-        dve.tensor_copy(T.osb[:], T.o0[:, 0:128]).then_inc(S.os0, 1)
+    o_last, ev_o, ev_L, g_last = T.o0, S.go0, S.ex0, 0
+    dve.wait_ge(S.zer, 1)
+    if r > 0:
+        dve.wait_ge(S.go0, 1)
+        dve.tensor_copy(cols(T.osb, 0, 1), T.o0[:, 0:128]).then_inc(S.gs0, 1)
 
         steps = list(range(1, r + 1))
-        head = steps[:-1]
-        chunks = [head[i:i + 2] for i in range(0, len(head), 2)] + [steps[-1:]]
-        nc = len(chunks)
-        STB = [T.st1, T.st2, T.st0]
-        TRB = [T.tr1, T.tr2, T.tr0]
+        n2 = min(3, r)
+        E, F = steps[:-n2], steps[-n2:]
+        gE, gF = (1, 2) if E else (None, 1)
+        chunks = []
+        if E:
+            chunks.append((T.st1, E))
+        if len(F) > 1:
+            chunks.append((T.st2, F[:-1]))
+        chunks.append((T.st0, F[-1:]))
+        TRB = [T.tr0, T.tr1, T.tr2]
+        OO = [T.o0, T.o1]
+        st_of = {}
 
-        for c, ch in enumerate(chunks):
-            if STB[c] is T.st0:
+        for c, (bank, ch) in enumerate(chunks):
+            if bank is T.st0:
                 pe.wait_ge(S.m0, 1)
             for i, t in enumerate(ch):
                 j = r - t
+                st_of[t] = cols(bank, i, 1)
                 pe.wait_ge(S["arr%d" % j], engines(send_mask(j)))
-                pe.matmul(cols(STB[c], i, 1), T.qs[:], kcol(j), True, True).then_inc(S["sc%d" % c], 1)
-            dve.wait_ge(S["sc%d" % c], len(ch))
-            dve.tensor_reduce(col(T.nb, 1 + c), cols(STB[c], 0, len(ch)), X, AluOpType.max,
-                              negate=True).then_inc(S["rc%d" % c], 1)
-        for c in range(nc):
-            dve.wait_ge(S["rc%d" % c], 1)
+                pe.matmul(st_of[t], T.qn[:], kcol(j), True, True).then_inc(ev("sc", c), 1)
         dve.wait_ge(S.m0, 1)
-        dve.tensor_reduce(col(T.nM, 0), T.nb[:, 0:nc + 1], X, AluOpType.min).then_inc(S.mm, 1)
-        act.wait_ge(S.mm, 1)
-        for c, ch in enumerate(chunks):
-            act.activation(cols(T.pt, ch[0], len(ch)), cols(STB[c], 0, len(ch)), EXP, bias=col(T.nM, 0), scale=1.0,
-                           accum_out=col(T.lv, c)).then_inc(S["pc%d" % c], 1)
-            if c == 0:
-                act.activation(col(T.av, 0), col(T.nb, 0), EXP, bias=col(T.nM, 0), scale=-1.0).then_inc(S.aa, 1)
-            if c == min(1, nc - 1):
-                act.wait_ge(S.aa, 1)
-                act.activation(col(T.lv, nc), col(T.L0, 0), IDENT, scale=col(T.av, 0)).then_inc(S.al, 1)
-        for c, ch in enumerate(chunks):
-            pe.wait_ge(S["pc%d" % c], 1)
-            for i, t in enumerate(ch):
-                pe.transpose(cols(TRB[c], i, 1), cols(T.pt, t, 1), T.ident[:]).then_inc(S["tc%d" % c], 1)
-        dve.wait_ge(S.aa, 1)
-        dve.wait_ge(S.idn, 1)
-        dve.tensor_scalar(T.da[:], T.ident[:], col(T.av, 0), None, AluOpType.mult).then_inc(S.dd, 1)
-        for c, ch in enumerate(chunks):
-            q = act if c == nc - 1 else dve
-            q.wait_ge(S["tc%d" % c], len(ch))
-            if c == nc - 1:
-                act.activation(cols(T.pp, ch[0], len(ch)), cols(TRB[c], 0, len(ch)), COPY).then_inc(S["cc%d" % c], 1)
+        prev = col(T.nb, 0)
+        neg_of = []
+        for c, (bank, ch) in enumerate(chunks):
+            n = 128 * len(ch)
+            out = T.scn[:, c * 256:c * 256 + n]
+            dve.wait_ge(ev("sc", c), len(ch))
+            if E and c == 1:
+                dve.tensor_reduce(col(T.nb, 1), bank[:, 0:n], X, MIN).then_inc(ev("rc", c), 1)
+                neg_of.append(col(T.nb, 1))
+                continue
+            if E and c == 2:
+                n0 = 128 * len(E)
+                dve.wait_ge(ev("rc", 0), 1)
+                dve.wait_ge(ev("rc", 1), 1)
+                dve.tensor_tensor_scan(out, bank[:, 0:n], T.scn[:, n0 - 128:n0], col(T.nb, 1),
+                                       MIN, MIN).then_inc(ev("rc", c), 1)
             else:
-                dve.tensor_copy(cols(T.pp, ch[0], len(ch)), cols(TRB[c], 0, len(ch))).then_inc(S["cc%d" % c], 1)
-        pe.wait_ge(S.dd, 1)
-        pe.wait_ge(S.os0, 1)
-        pe.matmul(T.o1[:, 0:128], T.da[:], T.osb[:], True, False)
-        for c, ch in enumerate(chunks):
-            pe.wait_ge(S["cc%d" % c], 1)
-            for t in ch:
-                mmi = pe.matmul(T.o1[:, 0:128], cols(T.pp, t, 1), vcol(r - t), False, t == r)
-                if t == r:
-                    mmi.then_inc(S.og1, 1)
-        for c in range(nc):
-            dve.wait_ge(S["pc%d" % c], 1)
-        dve.wait_ge(S.al, 1)
-        dve.tensor_reduce(col(T.Lf, 0), T.lv[:, 0:nc + 1], X, AluOpType.add).then_inc(S.ls, 1)
-        dve.wait_ge(S.ls, 1)
-        dve.reciprocal(col(T.rl, 0), col(T.Lf, 0)).then_inc(S.rcp, 1)
-        dve.wait_ge(S.rcp, 1)
-        dve.wait_ge(S.og1, 1)
-        dve.tensor_scalar(T.ysb[:], T.o1[:, 0:128], col(T.rl, 0), None, AluOpType.mult).then_inc(S.yy, 1)
+                if c > 0:
+                    dve.wait_ge(ev("rc", c - 1), 1)
+                dve.tensor_tensor_scan(out, bank[:, 0:n], T.zz[:, 0:n], prev, MIN, ADD).then_inc(ev("rc", c), 1)
+            prev = T.scn[:, c * 256 + n - 1:c * 256 + n]
+            neg_of.append(prev)
 
+        def act_group(gi, grp, c_shift, neg_prev, ev_Lprev):
+            neg = neg_of[c_shift]
+            act.wait_ge(ev("rc", c_shift), 1)
+            for i, t in enumerate(grp):
+                act.activation(cols(T.pt, t, 1), st_of[t], EXP, bias=neg, scale=-1.0,
+                               accum_out=col(T.lv, 8 * gi + i)).then_inc(ev("ex", t), 1)
+                if i == 0:
+                    act.activation(col(T.av, gi), neg_prev, EXP, bias=neg, scale=-1.0).then_inc(ev("ga", gi), 1)
+            act.wait_ge(ev("ga", gi), 1)
+            act.wait_ge(ev_Lprev, 1)
+            act.activation(col(T.lv, 8 * gi + len(grp)), col(T.Lg, gi - 1), IDENT,
+                           scale=col(T.av, gi)).then_inc(ev("gl", gi), 1)
+            act.wait_ge(S.idn, 1)
+            act.activation(cols(T.da, gi, 1), T.ident[:], IDENT, scale=col(T.av, gi)).then_inc(ev("gd", gi), 1)
+
+        def pe_tr(t):
+            pe.wait_ge(ev("ex", t), 1)
+            pe.transpose(TRB[t % 3][:, 0:128], cols(T.pt, t, 1), T.ident[:]).then_inc(ev("tt", t), 1)
+
+        def pe_merge(gi, start, stop):
+            pe.wait_ge(ev("gd", gi), 1)
+            pe.wait_ge(ev("gs", gi - 1), 1)
+            return pe.matmul(OO[gi % 2][:, 0:128], cols(T.da, gi, 1), cols(T.osb, gi - 1, 1), start, stop)
+
+        def pe_pv(gi, t, start, stop):
+            pe.wait_ge(ev("cp", t), 1)
+            return pe.matmul(OO[gi % 2][:, 0:128], cols(T.pp, t, 1), vcol(r - t), start, stop)
+
+        def dve_copy(t):
+            dve.wait_ge(ev("tt", t), 1)
+            dve.tensor_copy(cols(T.pp, t, 1), TRB[t % 3][:, 0:128]).then_inc(ev("cp", t), 1)
+
+        def dve_sum(gi, grp):
+            for t in grp:
+                dve.wait_ge(ev("ex", t), 1)
+            dve.wait_ge(ev("gl", gi), 1)
+            dve.tensor_reduce(col(T.Lg, gi), T.lv[:, 8 * gi:8 * gi + len(grp) + 1], X, ADD).then_inc(ev("gL", gi), 1)
+
+        if E:
+            act_group(gE, E, 0, col(T.nb, 0), S.ex0)
+            act_group(gF, F, len(chunks) - 1, neg_of[0], ev("gL", gE))
+        else:
+            act_group(gF, F, len(chunks) - 1, col(T.nb, 0), S.ex0)
+        on_act = F[-1] if len(F) >= 2 else None
+        if on_act is not None:
+            act.wait_ge(ev("tt", on_act), 1)
+            act.activation(cols(T.pp, on_act, 1), TRB[on_act % 3][:, 0:128], COPY).then_inc(ev("cp", on_act), 1)
+
+        if E:
+            pe_merge(gE, True, False)
+            for t in E:
+                pe_tr(t)
+        for i in range(max(len(E), len(F))):
+            if i < len(F):
+                pe_tr(F[i])
+            if i < len(E):
+                mmi = pe_pv(gE, E[i], False, i == len(E) - 1)
+                if i == len(E) - 1:
+                    mmi.then_inc(ev("go", gE), 1)
+        if len(F) == 1:
+            pe_merge(gF, True, False)
+            pe_pv(gF, F[0], False, True).then_inc(ev("go", gF), 1)
+        else:
+            for i, t in enumerate(F[:-1]):
+                pe_pv(gF, t, i == 0, False)
+            pe_merge(gF, False, False)
+            pe_pv(gF, F[-1], False, True).then_inc(ev("go", gF), 1)
+
+        for t in E:
+            dve_copy(t)
+        if E:
+            dve_sum(gE, E)
+        dve_copy(F[0])
+        dve_sum(gF, F)
+        for t in F[1:]:
+            if t != on_act:
+                dve_copy(t)
+        if E:
+            dve.wait_ge(ev("go", gE), 1)
+            dve.tensor_copy(cols(T.osb, gE, 1), OO[gE % 2][:, 0:128]).then_inc(ev("gs", gE), 1)
+        o_last, ev_o, ev_L, g_last = OO[gF % 2], ev("go", gF), ev("gL", gF), gF
+
+    dve.wait_ge(ev_L, 1)
+    dve.reciprocal(col(T.rl, 0), col(T.Lg, g_last)).then_inc(S.rcp, 1)
+    dve.wait_ge(S.rcp, 1)
+    dve.wait_ge(ev_o, 1)
+    dve.tensor_scalar(T.ysb[:], o_last[:, 0:128], col(T.rl, 0), None, AluOpType.mult).then_inc(S.yy, 1)
     sp.wait_ge(S.yy, 1)
     sp.dma_start(T.y[:], T.ysb[:]).then_inc(S.sto, 16)
     sp.wait_ge(S.sto, 16)

@@ -32,8 +32,8 @@ SCRATCH = {
     "o0": ("psum", [128, 512], "float32"),
     "o1": ("psum", [128, 512], "float32"),
 }
-SEMAPHORES = (["iot", "idn", "msk", "zer", "qng", "kvl", "ql", "sent", "rcp", "yy", "sto", "s0", "m0"]
-              + ["arr%d" % j for j in range(NR)]
+SEMAPHORES = (["iot", "idn", "msk", "zer", "qng", "kl", "vl", "ql", "sent", "rcp", "yy", "sto", "s0", "m0"]
+              + [s + str(j) for s in ["ka", "va"] for j in range(NR)]
               + [s + str(t) for s in ["ex", "tt", "cp"] for t in range(NR)]
               + [s + str(c) for s in ["sc", "rc", "ga", "gl", "gd", "go", "gs", "gL"] for c in range(3)])
 
@@ -60,9 +60,6 @@ def rank_program(g, core, T, topo):
     def engines(m):
         return bin(m).count("1")
 
-    def slot(j):
-        return T.kv[:, j * SLOT:(j + 1) * SLOT]
-
     def kcol(j):
         return T.kv[:, j * SLOT:j * SLOT + 128]
 
@@ -78,9 +75,9 @@ def rank_program(g, core, T, topo):
     def ev(name, i):
         return S[name + str(i)]
 
-    sp.dma_start(kcol(r), T.k[:]).then_inc(S.kvl, 16)
-    act.dma_start(vcol(r), T.v[:]).then_inc(S.kvl, 16)
-    sp.dma_start(T.qs[:], T.q[:]).then_inc(S.ql, 16)
+    sp.dma_start(kcol(r), T.k[:]).then_inc(S.kl, 16)
+    act.dma_start(T.qs[:], T.q[:]).then_inc(S.ql, 16)
+    sp.dma_start(vcol(r), T.v[:]).then_inc(S.vl, 16)
 
     g.iota(T.dm[:], [[1, 128]], 0, -1, allow_small_or_imprecise_dtypes=True).then_inc(S.iot, 1)
     later = cores[r + 1:]
@@ -89,13 +86,17 @@ def rank_program(g, core, T, topo):
         for d in later:
             rid, pid, _se = topo.addr(d)
             ids.append(DstId(rid=rid, pnc=pid))
-        g.wait_ge(S.kvl, 32)
-        g.remote_dma_fused(
-            [RemoteDMATransfer(dst_ids=ids, dma_engine_mask=send_mask(r), remote_sem=S["arr%d" % r],
-                               srcs=[slot(r)], dsts=[slot(r) for _d in later])],
-            local_sem=S.sent)
+        for lsem, name, part in ((S.kl, "ka", kcol(r)), (S.vl, "va", vcol(r))):
+            g.wait_ge(lsem, 16)
+            g.remote_dma_fused(
+                [RemoteDMATransfer(dst_ids=ids, dma_engine_mask=send_mask(r), remote_sem=ev(name, r),
+                                   srcs=[part], dsts=[part for _d in later])],
+                local_sem=S.sent)
 
-    dve.memset(T.zz[:], 0.0).then_inc(S.zer, 1)
+    act.wait_ge(S.iot, 1)
+    for h in range(2):
+        act.activation(cols(T.zz, h, 1), T.dm[:], EXP, bias=-200.0, scale=0.0).then_inc(S.zer, 1)
+
     dve.wait_ge(S.iot, 1)
     dve.tensor_scalar(T.ident[:], T.dm[:], 0.0, None, AluOpType.is_equal).then_inc(S.idn, 1)
     dve.tensor_scalar(T.maskT[:], T.dm[:], 0.0, -30000.0, AluOpType.is_gt, AluOpType.mult).then_inc(S.msk, 1)
@@ -103,7 +104,7 @@ def rank_program(g, core, T, topo):
     dve.tensor_scalar(T.qn[:], T.qs[:], -1.0, None, AluOpType.mult).then_inc(S.qng, 1)
 
     st = T.st0[:, 0:128]
-    pe.wait_ge(S.kvl, 32)
+    pe.wait_ge(S.kl, 16)
     pe.wait_ge(S.ql, 16)
     pe.matmul(st, T.qs[:], kcol(r), True, False)
     pe.wait_ge(S.idn, 1)
@@ -119,11 +120,12 @@ def rank_program(g, core, T, topo):
     act.wait_ge(S.tt0, 1)
     act.activation(cols(T.pp, 0, 1), T.tr0[:, 0:128], COPY).then_inc(S.cp0, 1)
     pe.wait_ge(S.cp0, 1)
+    pe.wait_ge(S.vl, 16)
     pe.matmul(T.o0[:, 0:128], cols(T.pp, 0, 1), vcol(r), True, True).then_inc(S.go0, 1)
     pe.wait_ge(S.qng, 1)
 
     o_last, ev_o, ev_L, g_last = T.o0, S.go0, S.ex0, 0
-    dve.wait_ge(S.zer, 1)
+    dve.wait_ge(S.zer, 2)
     if r > 0:
         dve.wait_ge(S.go0, 1)
         dve.tensor_copy(cols(T.osb, 0, 1), T.o0[:, 0:128]).then_inc(S.gs0, 1)
@@ -148,7 +150,7 @@ def rank_program(g, core, T, topo):
             for i, t in enumerate(ch):
                 j = r - t
                 st_of[t] = cols(bank, i, 1)
-                pe.wait_ge(S["arr%d" % j], engines(send_mask(j)))
+                pe.wait_ge(ev("ka", j), engines(send_mask(j)))
                 pe.matmul(st_of[t], T.qn[:], kcol(j), True, True).then_inc(ev("sc", c), 1)
         dve.wait_ge(S.m0, 1)
         prev = col(T.nb, 0)
@@ -191,6 +193,8 @@ def rank_program(g, core, T, topo):
 
         def pe_tr(t):
             pe.wait_ge(ev("ex", t), 1)
+            if t - 3 >= 1:
+                pe.wait_ge(ev("cp", t - 3), 1)
             pe.transpose(TRB[t % 3][:, 0:128], cols(T.pt, t, 1), T.ident[:]).then_inc(ev("tt", t), 1)
 
         def pe_merge(gi, start, stop):
@@ -200,6 +204,7 @@ def rank_program(g, core, T, topo):
 
         def pe_pv(gi, t, start, stop):
             pe.wait_ge(ev("cp", t), 1)
+            pe.wait_ge(ev("va", r - t), engines(send_mask(r - t)))
             return pe.matmul(OO[gi % 2][:, 0:128], cols(T.pp, t, 1), vcol(r - t), start, stop)
 
         def dve_copy(t):
@@ -265,4 +270,4 @@ def rank_program(g, core, T, topo):
     sp.dma_start(T.y[:], T.ysb[:]).then_inc(S.sto, 16)
     sp.wait_ge(S.sto, 16)
     if later:
-        g.wait_ge(S.sent, engines(send_mask(r)))
+        g.wait_ge(S.sent, 2 * engines(send_mask(r)))

from concourse.bass import DstId, RemoteDMATransfer
from concourse.mybir import AluOpType, AxisListType, ActivationFunctionType

NR = 6
SLOT = 256

SCRATCH = {
    "kv": ("sbuf", [128, NR * SLOT], "bfloat16"),
    "qs": ("sbuf", [128, 128], "bfloat16"),
    "qn": ("sbuf", [128, 128], "bfloat16"),
    "dm": ("sbuf", [128, 128], "bfloat16"),
    "ident": ("sbuf", [128, 128], "bfloat16"),
    "maskT": ("sbuf", [128, 128], "bfloat16"),
    "zz": ("sbuf", [128, 256], "float32"),
    "scn": ("sbuf", [128, 3 * 256], "float32"),
    "pt": ("sbuf", [128, NR * 128], "bfloat16"),
    "pp": ("sbuf", [128, NR * 128], "bfloat16"),
    "da": ("sbuf", [128, 3 * 128], "bfloat16"),
    "osb": ("sbuf", [128, 3 * 128], "bfloat16"),
    "ysb": ("sbuf", [128, 128], "bfloat16"),
    "nb": ("sbuf", [128, 4], "float32"),
    "av": ("sbuf", [128, 4], "float32"),
    "lv": ("sbuf", [128, 24], "float32"),
    "Lg": ("sbuf", [128, 4], "float32"),
    "rl": ("sbuf", [128, 4], "float32"),
    "st0": ("psum", [128, 512], "float32"),
    "st1": ("psum", [128, 512], "float32"),
    "st2": ("psum", [128, 512], "float32"),
    "tr0": ("psum", [128, 1024], "bfloat16"),
    "tr1": ("psum", [128, 1024], "bfloat16"),
    "tr2": ("psum", [128, 1024], "bfloat16"),
    "o0": ("psum", [128, 512], "float32"),
    "o1": ("psum", [128, 512], "float32"),
}
SEMAPHORES = (["iot", "idn", "msk", "zer", "qng", "kl", "vl", "ql", "sent", "rcp", "yy", "sto", "s0", "m0"]
              + [s + str(j) for s in ["ka", "va"] for j in range(NR)]
              + [s + str(t) for s in ["ex", "tt", "cp"] for t in range(NR)]
              + [s + str(c) for s in ["sc", "rc", "ga", "gl", "gd", "go", "gs", "gL"] for c in range(3)])


def rank_program(g, core, T, topo):
    r = T.rank_of(core)
    if r is None:
        return
    pe, dve, act, sp = g.tensor, g.vector, g.scalar, g.sync
    S = T.sem
    EXP, COPY, IDENT = ActivationFunctionType.Exp, ActivationFunctionType.Copy, ActivationFunctionType.Identity
    X = AxisListType.X
    MIN, ADD = AluOpType.min, AluOpType.add
    cores = list(T.cores)

    def send_mask(j):
        m = None
        for d in cores[j + 1:]:
            if not topo.may_write(cores[j], d):
                raise ValueError("rank %d may not write to core %d" % (j, d))
            m = topo.mask(cores[j], d) if m is None else (m & topo.mask(cores[j], d))
        return m

    def engines(m):
        return bin(m).count("1")

    def kcol(j):
        return T.kv[:, j * SLOT:j * SLOT + 128]

    def vcol(j):
        return T.kv[:, j * SLOT + 128:j * SLOT + 256]

    def cols(buf, a, n):
        return buf[:, a * 128:(a + n) * 128]

    def col(buf, t):
        return buf[:, t:t + 1]

    def ev(name, i):
        return S[name + str(i)]

    sp.dma_start(kcol(r), T.k[:]).then_inc(S.kl, 16)
    act.dma_start(T.qs[:], T.q[:]).then_inc(S.ql, 16)
    sp.dma_start(vcol(r), T.v[:]).then_inc(S.vl, 16)

    g.iota(T.dm[:], [[1, 128]], 0, -1, allow_small_or_imprecise_dtypes=True).then_inc(S.iot, 1)
    later = cores[r + 1:]
    if later:
        ids = []
        for d in later:
            rid, pid, _se = topo.addr(d)
            ids.append(DstId(rid=rid, pnc=pid))
        for lsem, name, part in ((S.kl, "ka", kcol(r)), (S.vl, "va", vcol(r))):
            g.wait_ge(lsem, 16)
            g.remote_dma_fused(
                [RemoteDMATransfer(dst_ids=ids, dma_engine_mask=send_mask(r), remote_sem=ev(name, r),
                                   srcs=[part], dsts=[part for _d in later])],
                local_sem=S.sent)

    act.wait_ge(S.iot, 1)
    for h in range(2):
        act.activation(cols(T.zz, h, 1), T.dm[:], EXP, bias=-200.0, scale=0.0).then_inc(S.zer, 1)

    dve.wait_ge(S.iot, 1)
    dve.tensor_scalar(T.ident[:], T.dm[:], 0.0, None, AluOpType.is_equal).then_inc(S.idn, 1)
    dve.tensor_scalar(T.maskT[:], T.dm[:], 0.0, -30000.0, AluOpType.is_gt, AluOpType.mult).then_inc(S.msk, 1)
    dve.wait_ge(S.ql, 16)
    dve.tensor_scalar(T.qn[:], T.qs[:], -1.0, None, AluOpType.mult).then_inc(S.qng, 1)

    st = T.st0[:, 0:128]
    pe.wait_ge(S.kl, 16)
    pe.wait_ge(S.ql, 16)
    pe.matmul(st, T.qs[:], kcol(r), True, False)
    pe.wait_ge(S.idn, 1)
    pe.wait_ge(S.msk, 1)
    pe.matmul(st, T.ident[:], T.maskT[:], False, True).then_inc(S.s0, 1)
    dve.wait_ge(S.s0, 1)
    dve.tensor_reduce(col(T.nb, 0), st, X, AluOpType.max, negate=True).then_inc(S.m0, 1)
    act.wait_ge(S.m0, 1)
    act.activation(cols(T.pt, 0, 1), st, EXP, bias=col(T.nb, 0), scale=1.0,
                   accum_out=col(T.Lg, 0)).then_inc(S.ex0, 1)
    pe.wait_ge(S.ex0, 1)
    pe.transpose(T.tr0[:, 0:128], cols(T.pt, 0, 1), T.ident[:]).then_inc(S.tt0, 1)
    act.wait_ge(S.tt0, 1)
    act.activation(cols(T.pp, 0, 1), T.tr0[:, 0:128], COPY).then_inc(S.cp0, 1)
    pe.wait_ge(S.cp0, 1)
    pe.wait_ge(S.vl, 16)
    pe.matmul(T.o0[:, 0:128], cols(T.pp, 0, 1), vcol(r), True, True).then_inc(S.go0, 1)
    pe.wait_ge(S.qng, 1)

    o_last, ev_o, ev_L, g_last = T.o0, S.go0, S.ex0, 0
    dve.wait_ge(S.zer, 2)
    if r > 0:
        dve.wait_ge(S.go0, 1)
        dve.tensor_copy(cols(T.osb, 0, 1), T.o0[:, 0:128]).then_inc(S.gs0, 1)

        steps = list(range(1, r + 1))
        n2 = min(3, r)
        E, F = steps[:-n2], steps[-n2:]
        gE, gF = (1, 2) if E else (None, 1)
        chunks = []
        if E:
            chunks.append((T.st1, E))
        if len(F) > 1:
            chunks.append((T.st2, F[:-1]))
        chunks.append((T.st0, F[-1:]))
        TRB = [T.tr0, T.tr1, T.tr2]
        OO = [T.o0, T.o1]
        st_of = {}

        for c, (bank, ch) in enumerate(chunks):
            if bank is T.st0:
                pe.wait_ge(S.m0, 1)
            for i, t in enumerate(ch):
                j = r - t
                st_of[t] = cols(bank, i, 1)
                pe.wait_ge(ev("ka", j), engines(send_mask(j)))
                pe.matmul(st_of[t], T.qn[:], kcol(j), True, True).then_inc(ev("sc", c), 1)
        dve.wait_ge(S.m0, 1)
        prev = col(T.nb, 0)
        neg_of = []
        for c, (bank, ch) in enumerate(chunks):
            n = 128 * len(ch)
            out = T.scn[:, c * 256:c * 256 + n]
            dve.wait_ge(ev("sc", c), len(ch))
            if E and c == 1:
                dve.tensor_reduce(col(T.nb, 1), bank[:, 0:n], X, MIN).then_inc(ev("rc", c), 1)
                neg_of.append(col(T.nb, 1))
                continue
            if E and c == 2:
                n0 = 128 * len(E)
                dve.wait_ge(ev("rc", 0), 1)
                dve.wait_ge(ev("rc", 1), 1)
                dve.tensor_tensor_scan(out, bank[:, 0:n], T.scn[:, n0 - 128:n0], col(T.nb, 1),
                                       MIN, MIN).then_inc(ev("rc", c), 1)
            else:
                if c > 0:
                    dve.wait_ge(ev("rc", c - 1), 1)
                dve.tensor_tensor_scan(out, bank[:, 0:n], T.zz[:, 0:n], prev, MIN, ADD).then_inc(ev("rc", c), 1)
            prev = T.scn[:, c * 256 + n - 1:c * 256 + n]
            neg_of.append(prev)

        def act_group(gi, grp, c_shift, neg_prev, ev_Lprev):
            neg = neg_of[c_shift]
            act.wait_ge(ev("rc", c_shift), 1)
            for i, t in enumerate(grp):
                act.activation(cols(T.pt, t, 1), st_of[t], EXP, bias=neg, scale=-1.0,
                               accum_out=col(T.lv, 8 * gi + i)).then_inc(ev("ex", t), 1)
                if i == 0:
                    act.activation(col(T.av, gi), neg_prev, EXP, bias=neg, scale=-1.0).then_inc(ev("ga", gi), 1)
            act.wait_ge(ev("ga", gi), 1)
            act.wait_ge(ev_Lprev, 1)
            act.activation(col(T.lv, 8 * gi + len(grp)), col(T.Lg, gi - 1), IDENT,
                           scale=col(T.av, gi)).then_inc(ev("gl", gi), 1)
            act.wait_ge(S.idn, 1)
            act.activation(cols(T.da, gi, 1), T.ident[:], IDENT, scale=col(T.av, gi)).then_inc(ev("gd", gi), 1)

        def pe_tr(t):
            pe.wait_ge(ev("ex", t), 1)
            if t - 3 >= 1:
                pe.wait_ge(ev("cp", t - 3), 1)
            pe.transpose(TRB[t % 3][:, 0:128], cols(T.pt, t, 1), T.ident[:]).then_inc(ev("tt", t), 1)

        def pe_merge(gi, start, stop):
            pe.wait_ge(ev("gd", gi), 1)
            pe.wait_ge(ev("gs", gi - 1), 1)
            return pe.matmul(OO[gi % 2][:, 0:128], cols(T.da, gi, 1), cols(T.osb, gi - 1, 1), start, stop)

        def pe_pv(gi, t, start, stop):
            pe.wait_ge(ev("cp", t), 1)
            pe.wait_ge(ev("va", r - t), engines(send_mask(r - t)))
            return pe.matmul(OO[gi % 2][:, 0:128], cols(T.pp, t, 1), vcol(r - t), start, stop)

        def dve_copy(t):
            dve.wait_ge(ev("tt", t), 1)
            dve.tensor_copy(cols(T.pp, t, 1), TRB[t % 3][:, 0:128]).then_inc(ev("cp", t), 1)

        def dve_sum(gi, grp):
            for t in grp:
                dve.wait_ge(ev("ex", t), 1)
            dve.wait_ge(ev("gl", gi), 1)
            dve.tensor_reduce(col(T.Lg, gi), T.lv[:, 8 * gi:8 * gi + len(grp) + 1], X, ADD).then_inc(ev("gL", gi), 1)

        if E:
            act_group(gE, E, 0, col(T.nb, 0), S.ex0)
            act_group(gF, F, len(chunks) - 1, neg_of[0], ev("gL", gE))
        else:
            act_group(gF, F, len(chunks) - 1, col(T.nb, 0), S.ex0)
        on_act = F[-1] if len(F) >= 2 else None
        if on_act is not None:
            act.wait_ge(ev("tt", on_act), 1)
            act.activation(cols(T.pp, on_act, 1), TRB[on_act % 3][:, 0:128], COPY).then_inc(ev("cp", on_act), 1)

        if E:
            pe_merge(gE, True, False)
            for t in E:
                pe_tr(t)
        for i in range(max(len(E), len(F))):
            if i < len(F):
                pe_tr(F[i])
            if i < len(E):
                mmi = pe_pv(gE, E[i], False, i == len(E) - 1)
                if i == len(E) - 1:
                    mmi.then_inc(ev("go", gE), 1)
        if len(F) == 1:
            pe_merge(gF, True, False)
            pe_pv(gF, F[0], False, True).then_inc(ev("go", gF), 1)
        else:
            for i, t in enumerate(F[:-1]):
                pe_pv(gF, t, i == 0, False)
            pe_merge(gF, False, False)
            pe_pv(gF, F[-1], False, True).then_inc(ev("go", gF), 1)

        for t in E:
            dve_copy(t)
        if E:
            dve_sum(gE, E)
        dve_copy(F[0])
        dve_sum(gF, F)
        for t in F[1:]:
            if t != on_act:
                dve_copy(t)
        if E:
            dve.wait_ge(ev("go", gE), 1)
            dve.tensor_copy(cols(T.osb, gE, 1), OO[gE % 2][:, 0:128]).then_inc(ev("gs", gE), 1)
        o_last, ev_o, ev_L, g_last = OO[gF % 2], ev("go", gF), ev("gL", gF), gF

    dve.wait_ge(ev_L, 1)
    dve.reciprocal(col(T.rl, 0), col(T.Lg, g_last)).then_inc(S.rcp, 1)
    dve.wait_ge(S.rcp, 1)
    dve.wait_ge(ev_o, 1)
    dve.tensor_scalar(T.ysb[:], o_last[:, 0:128], col(T.rl, 0), None, AluOpType.mult).then_inc(S.yy, 1)
    sp.wait_ge(S.yy, 1)
    sp.dma_start(T.y[:], T.ysb[:]).then_inc(S.sto, 16)
    sp.wait_ge(S.sto, 16)
    if later:
        g.wait_ge(S.sent, 2 * engines(send_mask(r)))
